import numpy as np
import ml_dtypes


def mxq(x, axis, fmt="e4m3"):
    dtype, down = {"e4m3": (ml_dtypes.float8_e4m3fn, 7), "e5m2": (ml_dtypes.float8_e5m2, 14)}[fmt]
    v = np.moveaxis(np.asarray(x, np.float32).astype(ml_dtypes.bfloat16).astype(np.float64), axis, -1)
    blocks = v.reshape(v.shape[:-1] + (-1, 32))
    amax = np.abs(blocks).max(-1, keepdims=True)
    byte = np.maximum(np.where(amax > 0, np.frexp(amax)[1] - 1 + 127, 0) - down, 1)
    scale = np.exp2(byte - 127.0)
    codes = (blocks / scale).astype(np.float32).astype(dtype).astype(np.float64)
    return np.moveaxis((codes * scale).reshape(v.shape), -1, axis)


WIDE = False


def mx_kscale(k, group=512):
    if not WIDE:
        return np.ones(k)
    levels = np.array([10, -10, 5, -5, 0])
    if group != 512:
        return np.exp2(np.random.permutation(np.resize(levels, k // group))).repeat(group)
    if k % 512:
        return np.exp2(np.random.permutation(np.resize(levels, k // 32))).repeat(32)
    a = np.empty((k // 512, 16))
    for p in range(k // 512):
        a[p, :8] = np.random.permutation(np.resize(levels, 8))
        for g in range(8):
            far = levels[np.abs(levels - a[p, g]) >= 10]
            a[p, g + 8] = far[np.random.randint(len(far))]
    return np.exp2(a.ravel()).repeat(32)


def f64(x):
    return np.asarray(x).astype(np.float64)


def striped(idx):
    return np.tile(np.asarray(idx).reshape(-1, 16).T, (8, 1)).astype(np.uint16)


def unstriped(offs):
    return offs[:16].T.reshape(-1).astype(np.int64)


H, KV, D, NQ, N = 4, 1, 256, 512, 512
CAP = 2.0


def setup_inputs():
    n = np.random.standard_normal
    s = mx_kscale(D, 0)[:, None]
    u = mx_kscale(N)
    t = np.random.uniform(0.5, 2.0, N) * u
    v = n((KV, N, 128))
    return {
        "qT": (n((H, D, NQ)) * s * (0.70 / np.sqrt(D))).astype(np.float32),
        "kT": (n((KV, D, N)) / s).astype(np.float32),
        "t": t.reshape(N, 1).astype(np.float32),
        "v": (v / t[:, None]).astype(np.float32),
        "kb": (0.5 * n((N, 1))).astype(np.float32),
        "og": n((H, NQ, 128)).astype(np.float32),
    }


def reference(qT, kT, t, v, kb, og):
    a = np.repeat(mxq(f64(kT), 1, "e4m3"), H // KV, 0).transpose(0, 2, 1) @ mxq(f64(qT), 1, "e4m3")
    a = a + f64(kb)
    a = CAP * np.tanh(a / CAP)
    p = 1.0 / (1.0 + np.exp(-a))
    w = p * f64(t)
    y = mxq(w, 1, "e4m3").transpose(0, 2, 1) @ np.repeat(mxq(f64(v), 1, "e4m3"), H // KV, 0)
    y = y / 16.0
    y = y / (1.0 + np.exp(-f64(og)))
    return y

@@ -1,0 +1,250 @@
+from contextlib import ExitStack
+
+import concourse.mybir as mybir
+
+H, D, NQ, N, E = 4, 256, 512, 512, 128
+FLOPS = 2 * H * N * NQ * D + 2 * H * NQ * N * E
+
+F32 = mybir.dt.float32
+BF16 = mybir.dt.bfloat16
+U32 = mybir.dt.uint32
+U8 = mybir.dt.uint8
+FP8X4 = mybir.dt.float8_e4m3fn_x4
+ACT = mybir.ActivationFunctionType
+ALU = mybir.AluOpType
+
+P = 128
+ROWS = 64
+PACK = 4
+RUN = 4
+QB = 128
+
+
+def plan():
+    ops = [("small",)]
+    ops += [("ld_q", 0, 0, 1, 0, "sp"), ("ld_q", 0, 0, 1, 1, "act")]
+    ops += [("ld_k", 0, 80, 0, "sp"), ("ld_k", 0, 80, 1, "act"), ("ld_k", 80, 128, 0, "sp"), ("ld_k", 80, 128, 1, "act")]
+    ops += [("warm",)]
+    ops += [("ld_og", 0), ("ld_q", 0, 1, 2, 2, "sp"), ("ld_q", 0, 3, 1, 2, "sp"), ("ld_v",), ("ld_q", 1, 0, 2, 2, "sp"), ("ld_q", 1, 2, 2, 2, "sp")]
+    ops += [("ld_og", 1), ("ld_og", 2), ("ld_og", 3)]
+    ops += [("cp_q", 0, 0, 1), ("cp_k", 0, 80), ("cp_k", 80, 128), ("qz_q", 0, 0, 0, 1)]
+    ops += [("qz_k", 0, 1), ("qz_k", 1, 2), ("qz_k", 2, 4)]
+    ops += [("G", 0, 0, 4)]
+    ops += [("mm_s", 0, 0, 1, 0, 1), ("mm_s", 0, 0, 1, 1, 2), ("mm_s", 0, 0, 1, 2, 4), ("mm_s", 1, 0, 1, 0, 4)]
+    ops += [("cp_q", 0, 1, 2), ("cp_q", 0, 3, 1), ("qz_q", 0, 1, 1, 2), ("qz_q", 0, 3, 3, 1), ("cp_v",)]
+    ops += [("T", 0, 0, 1, r) for r in range(4)]
+    ops += [("T", 1, 0, 1, 0), ("S", 0, 0, 1), ("W", 0, 0, 1), ("qz_v",)]
+    ops += [("mm_s", 0, 1, 3, r, r + 1) for r in range(3)]
+    ops += [("T", 1, 0, 1, r) for r in range(1, 4)]
+    ops += [("T", 0, 1, 3, 0), ("mm_s", 0, 1, 3, 3, 4), ("S", 1, 0, 1), ("cp_q", 1, 0, 2), ("Q", 0, 0, 1), ("W", 1, 0, 1)]
+    ops += [("mm_s", 1, 1, 3, 0, 1), ("mm_s", 1, 1, 3, 1, 2), ("mm_s", 1, 1, 3, 2, 3)]
+    ops += [("T", 0, 1, 3, r) for r in range(1, 4)]
+    ops += [("qz_q", 1, 0, 0, 2), ("Q", 1, 0, 1), ("cp_q", 1, 2, 2)]
+    ops += [("T", 1, 1, 3, 0), ("mm_s", 1, 1, 3, 3, 4), ("S", 0, 1, 1), ("W", 0, 1, 1), ("qz_q", 1, 2, 2, 2)]
+    ops += [("T", 1, 1, 3, 1), ("S", 0, 2, 1), ("Q", 0, 1, 1), ("W", 0, 2, 1)]
+    ops += [("mm_s", 2, 0, 4, r, r + 1) for r in range(3)]
+    ops += [("T", 1, 1, 3, 2), ("S", 0, 3, 1), ("W", 0, 3, 1), ("Q", 0, 2, 1)]
+    ops += [("T", 1, 1, 3, 3), ("T", 2, 0, 4, 0), ("mm_s", 2, 0, 4, 3, 4), ("S", 1, 1, 1), ("W", 1, 1, 1), ("Q", 0, 3, 1)]
+    ops += [("mm_s", 3, 0, 2, 0, 2), ("mm_s", 3, 0, 2, 2, 4), ("mm_s", 3, 2, 1, 0, 4)]
+    ops += [("mm_y", 0, 0, b) for b in range(4)]
+    ops += [("T", 2, 0, 4, 1), ("S", 1, 2, 1), ("W", 1, 2, 1), ("Q", 1, 1, 1), ("F", 0, 0, 4)]
+    ops += [("T", 2, 0, 4, 2), ("S", 1, 3, 1), ("W", 1, 3, 1), ("Q", 1, 2, 1)]
+    ops += [("T", 2, 0, 4, 3), ("G", 1, 0, 4), ("T", 3, 0, 2, 0), ("S", 2, 0, 1), ("W", 2, 0, 1), ("Q", 1, 3, 1)]
+    ops += [("mm_y", 1, 0, b) for b in range(4)]
+    ops += [("T", 3, 0, 2, 1), ("mm_s", 3, 3, 1, 0, 4), ("T", 3, 0, 2, 2), ("S", 2, 1, 1), ("W", 2, 1, 1), ("Q", 2, 0, 1), ("F", 1, 0, 4)]
+    ops += [("T", 3, 0, 2, 3), ("T", 3, 2, 1, 0), ("T", 3, 2, 1, 1), ("S", 2, 2, 1), ("W", 2, 2, 1), ("Q", 2, 1, 1)]
+    ops += [("T", 3, 2, 1, 2), ("T", 3, 2, 1, 3), ("S", 2, 3, 1), ("W", 2, 3, 1), ("Q", 2, 2, 1)]
+    ops += [("G", 2, 0, 4), ("S", 3, 0, 1), ("W", 3, 0, 1), ("Q", 2, 3, 1)]
+    ops += [("mm_y", 2, 0, b) for b in range(4)]
+    ops += [("T", 3, 3, 1, 0), ("T", 3, 3, 1, 1), ("S", 3, 1, 1), ("W", 3, 1, 1), ("Q", 3, 0, 1), ("F", 2, 0, 4)]
+    ops += [("T", 3, 3, 1, 2), ("T", 3, 3, 1, 3), ("S", 3, 2, 1), ("W", 3, 2, 1), ("Q", 3, 1, 1)]
+    ops += [("mm_y", 3, 0, 0), ("mm_y", 3, 0, 1)]
+    ops += [("S", 3, 3, 1), ("G", 3, 0, 4), ("W", 3, 3, 1), ("Q", 3, 2, 1), ("mm_y", 3, 2, 2), ("F", 3, 0, 2), ("Q", 3, 3, 1)]
+    ops += [("mm_y", 3, 3, 3), ("F", 3, 2, 1), ("F", 3, 3, 1)]
+    return ops
+
+
+def tile_rows_a_sigmoid_kb_cap_gate_kernel(tc, qT, kT, t, v, kb, og, out):
+    nc = tc.nc
+    with ExitStack() as ctx:
+        sb = ctx.enter_context(tc.tile_pool(name="sb", bufs=1))
+        score_pools = [ctx.enter_context(tc.psum_pool(name="scores%d" % g, bufs=3)) for g in range(2)]
+        y_pool = ctx.enter_context(tc.psum_pool(name="y", bufs=2))
+        ctx.enter_context(tc.manual_schedule())
+        tiles = {}
+
+        def new(key, shape, dtype):
+            tiles[key] = sb.tile(shape, dtype, name="_".join([str(x) for x in key]), align_bytes=64)
+            return tiles[key]
+
+        def engine(name):
+            return {"sp": nc.sync, "act": nc.scalar, "pool": nc.gpsimd}[name]
+
+        k_codes = new(("k_codes",), [P, N], U32)
+        k_scales = new(("k_scales",), [P, N], U8)
+        k_words = new(("k_words",), [P, PACK, P, PACK], BF16)
+        q_of_block = {}
+        u_of_block = {}
+        y_of_block = {}
+        banks = {}
+
+        def quantize(codes, scales, words):
+            nc.vector.quantize_mx(out=codes.bitcast(FP8X4), scales=scales, in_=words)
+
+        for op in plan():
+            kind = op[0]
+            if kind == "small":
+                t_col = new(("t",), [P, PACK], F32)
+                kb_col = new(("kb",), [P, PACK], F32)
+                kb_half = new(("kbh",), [P, PACK], F32)
+                nc.gpsimd.dma_start(out=kb_col[:], in_=kb.rearrange("(s r) o -> s (r o)", r=PACK))
+                nc.gpsimd.dma_start(out=t_col[:], in_=t.rearrange("(s r) o -> s (r o)", r=PACK))
+                nc.gpsimd.tensor_scalar(out=kb_half[:], in0=kb_col[:], scalar1=0.5, scalar2=0.0, op0=ALU.mult, op1=ALU.add)
+            elif kind == "warm":
+                warm_in = new(("warm_in",), [P, 1], F32)
+                warm_out = new(("warm_out",), [P, 1], F32)
+                nc.vector.memset(warm_in[:], 0.0)
+                nc.scalar.activation(out=warm_out[:], in_=warm_in[:], func=ACT.Sigmoid)
+            elif kind == "ld_q":
+                pair, b0, nb, g, eng = op[1:]
+                key = ("q_raw", pair, b0)
+                raw = tiles[key] if key in tiles else new(key, [P, PACK, nb * QB], F32)
+                cols = slice(b0 * QB, (b0 + nb) * QB)
+                if g == 2:
+                    src = qT[2 * pair : 2 * pair + 2, :, cols].rearrange("h (p j) q -> (h p) j q", j=PACK)
+                    engine(eng).dma_start(out=raw[:], in_=src)
+                else:
+                    src = qT[2 * pair + g, :, cols].rearrange("(p j) q -> p j q", j=PACK)
+                    engine(eng).dma_start(out=raw[ROWS * g : ROWS * (g + 1)], in_=src)
+            elif kind == "ld_k":
+                s0, s1, g, eng = op[1:]
+                key = ("k_raw", s0)
+                raw = tiles[key] if key in tiles else new(key, [P, PACK, (s1 - s0) * PACK], F32)
+                src = kT[0, :, s0 * PACK : s1 * PACK].rearrange("(p j) i -> p j i", j=PACK)
+                engine(eng).dma_start(out=raw[ROWS * g : ROWS * (g + 1)], in_=src)
+            elif kind == "ld_v":
+                raw = new(("v_raw",), [P, PACK, E], F32)
+                nc.sync.dma_start(out=raw[:], in_=v[0].rearrange("(s r) e -> s r e", r=PACK))
+            elif kind == "ld_og":
+                h = op[1]
+                raw = new(("og", h), [P, NQ // QB, E], F32)
+                nc.sync.dma_start(out=raw[:], in_=og[h].rearrange("(b p) e -> p b e", p=QB))
+            elif kind == "cp_k":
+                s0, s1 = op[1:]
+                raw = tiles[("k_raw", s0)]
+                nc.vector.tensor_copy(
+                    out=k_words[:, :, s0:s1, :].rearrange("p r s j -> p s j r"),
+                    in_=raw[:].rearrange("p j (s r) -> p s j r", r=PACK),
+                )
+            elif kind == "qz_k":
+                r0, r1 = op[1:]
+                cols = slice(r0 * P, r1 * P)
+                quantize(k_codes[:, cols], k_scales[:, cols], k_words[:, r0:r1].rearrange("p r s j -> p (r s j)"))
+            elif kind == "cp_q":
+                pair, b0, nb = op[1:]
+                raw = tiles[("q_raw", pair, b0)]
+                words = new(("q_words", pair, b0), [P, nb * QB, PACK], BF16)
+                nc.vector.tensor_copy(
+                    out=words[:].rearrange("p (c i) j -> p c j i", i=RUN),
+                    in_=raw[:].rearrange("p j (c i) -> p c j i", i=RUN),
+                )
+            elif kind == "qz_q":
+                pair, c0, b0, nb = op[1:]
+                words = tiles[("q_words", pair, c0)]
+                codes = new(("q_codes", pair, b0), [P, nb * QB], U32)
+                scales = new(("q_scales", pair, b0), [P, nb * QB], U8)
+                quantize(codes[:], scales[:], words[:, (b0 - c0) * QB : (b0 - c0 + nb) * QB, :].rearrange("p q j -> p (q j)"))
+                for b in range(nb):
+                    q_of_block[(pair, b0 + b)] = (codes, scales, slice(b * QB, (b + 1) * QB))
+            elif kind == "cp_v":
+                words = new(("v_words",), [P, E, PACK], BF16)
+                nc.vector.tensor_copy(
+                    out=words[:].rearrange("p (c i) r -> p c r i", i=RUN),
+                    in_=tiles[("v_raw",)][:].rearrange("p r (c i) -> p c r i", i=RUN),
+                )
+            elif kind == "qz_v":
+                v_codes = new(("v_codes",), [P, E], U32)
+                v_scales = new(("v_scales",), [P, E], U8)
+                quantize(v_codes[:], v_scales[:], tiles[("v_words",)][:].rearrange("p e r -> p (e r)"))
+            elif kind == "mm_s":
+                h, b0, nb, r0, r1 = op[1:]
+                g = h % 2
+                rows = slice(ROWS * g, ROWS * (g + 1))
+                bank = score_pools[g].tile([P, NQ], F32, name="bank", tag="bank")
+                for r in range(r0, r1):
+                    banks[(h, b0, r)] = bank[:, (r - r0) * nb * QB : (r - r0 + 1) * nb * QB]
+                    for b in range(nb):
+                        codes, scales, cols = q_of_block[(h // 2, b0 + b)]
+                        at = ((r - r0) * nb + b) * QB
+                        nc.tensor.matmul_mx(
+                            out=bank[:, at : at + QB],
+                            lhsT=k_codes[rows, r * P : (r + 1) * P].bitcast(FP8X4),
+                            lhsT_scale=k_scales[rows, r * P : (r + 1) * P],
+                            rhs=codes[rows, cols].bitcast(FP8X4),
+                            rhs_scale=scales[rows, cols],
+                            start=True,
+                            stop=True,
+                        )
+            elif kind == "T":
+                h, b0, nb, r = op[1:]
+                key = ("u", h, b0)
+                u = tiles[key] if key in tiles else new(key, [P, PACK, nb * QB], F32)
+                for b in range(nb):
+                    u_of_block[(h, b0 + b)] = (u, b * QB)
+                nc.scalar.activation(
+                    out=u[:, r, :], in_=banks[(h, b0, r)], func=ACT.Tanh, bias=tiles[("kbh",)][:, r : r + 1], scale=0.5
+                )
+            elif kind == "S":
+                h, b0, nb = op[1:]
+                u, at = u_of_block[(h, b0)]
+                p = new(("p", h, b0), [P, PACK, nb * QB], F32)
+                nc.scalar.activation(out=p[:], in_=u[:, :, at : at + nb * QB], func=ACT.Sigmoid, scale=2.0)
+            elif kind == "G":
+                h, b0, nb = op[1:]
+                key = ("gate", h)
+                gate = tiles[key] if key in tiles else new(key, [P, NQ // QB, E], F32)
+                nc.scalar.activation(out=gate[:, b0 : b0 + nb], in_=tiles[("og", h)][:, b0 : b0 + nb], func=ACT.Sigmoid)
+            elif kind == "W":
+                h, b0, nb = op[1:]
+                words = new(("w_words", h, b0), [P, nb * QB, PACK], BF16)
+                nc.vector.tensor_tensor(
+                    out=words[:].rearrange("p (c i) r -> p c r i", i=RUN),
+                    in0=tiles[("p", h, b0)][:].rearrange("p r (c i) -> p c r i", i=RUN),
+                    in1=tiles[("t",)][:].unsqueeze(1).unsqueeze(3).to_broadcast([P, nb * QB // RUN, PACK, RUN]),
+                    op=ALU.mult,
+                )
+            elif kind == "Q":
+                h, b0, nb = op[1:]
+                codes = new(("w_codes", h, b0), [P, nb * QB], U32)
+                scales = new(("w_scales", h, b0), [P, nb * QB], U8)
+                quantize(codes[:], scales[:], tiles[("w_words", h, b0)][:].rearrange("p q r -> p (q r)"))
+                for b in range(nb):
+                    tiles[("w", h, b0 + b)] = (codes, scales, slice(b * QB, (b + 1) * QB))
+            elif kind == "mm_y":
+                h, f0, b = op[1:]
+                if b == f0:
+                    y_of_block[(h, f0)] = y_pool.tile([P, NQ // QB, E], F32, name="y", tag="y")
+                codes, scales, cols = tiles[("w", h, b)]
+                nc.tensor.matmul_mx(
+                    out=y_of_block[(h, f0)][:, b - f0, :],
+                    lhsT=codes[:, cols].bitcast(FP8X4),
+                    lhsT_scale=scales[:, cols],
+                    rhs=tiles[("v_codes",)][:].bitcast(FP8X4),
+                    rhs_scale=tiles[("v_scales",)][:],
+                    start=True,
+                    stop=True,
+                )
+            elif kind == "F":
+                h, f0, nb = op[1:]
+                res = new(("res", h, f0), [P, nb, E], F32)
+                nc.vector.scalar_tensor_tensor(
+                    out=res[:],
+                    in0=y_of_block[(h, f0)][:, 0:nb, :],
+                    scalar=1.0 / 16.0,
+                    in1=tiles[("gate", h)][:, f0 : f0 + nb, :],
+                    op0=ALU.mult,
+                    op1=ALU.mult,
+                )
+                nc.sync.dma_start(
+                    out=out[h, f0 * QB : (f0 + nb) * QB, :].rearrange("(b p) e -> p b e", p=QB), in_=res[:]
+                )

@@ -7,6 +7,7 @@ FLOPS = 2 * H * N * NQ * D + 2 * H * NQ * N * E
 
 F32 = mybir.dt.float32
 BF16 = mybir.dt.bfloat16
+I32 = mybir.dt.int32
 U32 = mybir.dt.uint32
 U8 = mybir.dt.uint8
 FP8X4 = mybir.dt.float8_e4m3fn_x4
@@ -14,237 +15,298 @@ ACT = mybir.ActivationFunctionType
 ALU = mybir.AluOpType
 
 P = 128
-ROWS = 64
+ROWS = D // 4
 PACK = 4
-RUN = 4
 QB = 128
-
-
-def plan():
-    ops = [("small",)]
-    ops += [("ld_q", 0, 0, 1, 0, "sp"), ("ld_q", 0, 0, 1, 1, "act")]
-    ops += [("ld_k", 0, 80, 0, "sp"), ("ld_k", 0, 80, 1, "act"), ("ld_k", 80, 128, 0, "sp"), ("ld_k", 80, 128, 1, "act")]
-    ops += [("warm",)]
-    ops += [("ld_og", 0), ("ld_q", 0, 1, 2, 2, "sp"), ("ld_q", 0, 3, 1, 2, "sp"), ("ld_v",), ("ld_q", 1, 0, 2, 2, "sp"), ("ld_q", 1, 2, 2, 2, "sp")]
-    ops += [("ld_og", 1), ("ld_og", 2), ("ld_og", 3)]
-    ops += [("cp_q", 0, 0, 1), ("cp_k", 0, 80), ("cp_k", 80, 128), ("qz_q", 0, 0, 0, 1)]
-    ops += [("qz_k", 0, 1), ("qz_k", 1, 2), ("qz_k", 2, 4)]
-    ops += [("G", 0, 0, 4)]
-    ops += [("mm_s", 0, 0, 1, 0, 1), ("mm_s", 0, 0, 1, 1, 2), ("mm_s", 0, 0, 1, 2, 4), ("mm_s", 1, 0, 1, 0, 4)]
-    ops += [("cp_q", 0, 1, 2), ("cp_q", 0, 3, 1), ("qz_q", 0, 1, 1, 2), ("qz_q", 0, 3, 3, 1), ("cp_v",)]
-    ops += [("T", 0, 0, 1, r) for r in range(4)]
-    ops += [("T", 1, 0, 1, 0), ("S", 0, 0, 1), ("W", 0, 0, 1), ("qz_v",)]
-    ops += [("mm_s", 0, 1, 3, r, r + 1) for r in range(3)]
-    ops += [("T", 1, 0, 1, r) for r in range(1, 4)]
-    ops += [("T", 0, 1, 3, 0), ("mm_s", 0, 1, 3, 3, 4), ("S", 1, 0, 1), ("cp_q", 1, 0, 2), ("Q", 0, 0, 1), ("W", 1, 0, 1)]
-    ops += [("mm_s", 1, 1, 3, 0, 1), ("mm_s", 1, 1, 3, 1, 2), ("mm_s", 1, 1, 3, 2, 3)]
-    ops += [("T", 0, 1, 3, r) for r in range(1, 4)]
-    ops += [("qz_q", 1, 0, 0, 2), ("Q", 1, 0, 1), ("cp_q", 1, 2, 2)]
-    ops += [("T", 1, 1, 3, 0), ("mm_s", 1, 1, 3, 3, 4), ("S", 0, 1, 1), ("W", 0, 1, 1), ("qz_q", 1, 2, 2, 2)]
-    ops += [("T", 1, 1, 3, 1), ("S", 0, 2, 1), ("Q", 0, 1, 1), ("W", 0, 2, 1)]
-    ops += [("mm_s", 2, 0, 4, r, r + 1) for r in range(3)]
-    ops += [("T", 1, 1, 3, 2), ("S", 0, 3, 1), ("W", 0, 3, 1), ("Q", 0, 2, 1)]
-    ops += [("T", 1, 1, 3, 3), ("T", 2, 0, 4, 0), ("mm_s", 2, 0, 4, 3, 4), ("S", 1, 1, 1), ("W", 1, 1, 1), ("Q", 0, 3, 1)]
-    ops += [("mm_s", 3, 0, 2, 0, 2), ("mm_s", 3, 0, 2, 2, 4), ("mm_s", 3, 2, 1, 0, 4)]
-    ops += [("mm_y", 0, 0, b) for b in range(4)]
-    ops += [("T", 2, 0, 4, 1), ("S", 1, 2, 1), ("W", 1, 2, 1), ("Q", 1, 1, 1), ("F", 0, 0, 4)]
-    ops += [("T", 2, 0, 4, 2), ("S", 1, 3, 1), ("W", 1, 3, 1), ("Q", 1, 2, 1)]
-    ops += [("T", 2, 0, 4, 3), ("G", 1, 0, 4), ("T", 3, 0, 2, 0), ("S", 2, 0, 1), ("W", 2, 0, 1), ("Q", 1, 3, 1)]
-    ops += [("mm_y", 1, 0, b) for b in range(4)]
-    ops += [("T", 3, 0, 2, 1), ("mm_s", 3, 3, 1, 0, 4), ("T", 3, 0, 2, 2), ("S", 2, 1, 1), ("W", 2, 1, 1), ("Q", 2, 0, 1), ("F", 1, 0, 4)]
-    ops += [("T", 3, 0, 2, 3), ("T", 3, 2, 1, 0), ("T", 3, 2, 1, 1), ("S", 2, 2, 1), ("W", 2, 2, 1), ("Q", 2, 1, 1)]
-    ops += [("T", 3, 2, 1, 2), ("T", 3, 2, 1, 3), ("S", 2, 3, 1), ("W", 2, 3, 1), ("Q", 2, 2, 1)]
-    ops += [("G", 2, 0, 4), ("S", 3, 0, 1), ("W", 3, 0, 1), ("Q", 2, 3, 1)]
-    ops += [("mm_y", 2, 0, b) for b in range(4)]
-    ops += [("T", 3, 3, 1, 0), ("T", 3, 3, 1, 1), ("S", 3, 1, 1), ("W", 3, 1, 1), ("Q", 3, 0, 1), ("F", 2, 0, 4)]
-    ops += [("T", 3, 3, 1, 2), ("T", 3, 3, 1, 3), ("S", 3, 2, 1), ("W", 3, 2, 1), ("Q", 3, 1, 1)]
-    ops += [("mm_y", 3, 0, 0), ("mm_y", 3, 0, 1)]
-    ops += [("S", 3, 3, 1), ("G", 3, 0, 4), ("W", 3, 3, 1), ("Q", 3, 2, 1), ("mm_y", 3, 2, 2), ("F", 3, 0, 2), ("Q", 3, 3, 1)]
-    ops += [("mm_y", 3, 3, 3), ("F", 3, 2, 1), ("F", 3, 3, 1)]
-    return ops
+BLOCKS = NQ // QB
+BANK = 512
+SCORE_BANKS = 3
+K_PIECES = ((0, 64), (64, 104), (104, 128))
+COPY_RUN = 4
+WEIGHT_RUN = 2
 
 
 def tile_rows_a_sigmoid_kb_cap_gate_kernel(tc, qT, kT, t, v, kb, og, out):
     nc = tc.nc
     with ExitStack() as ctx:
         sb = ctx.enter_context(tc.tile_pool(name="sb", bufs=1))
-        score_pools = [ctx.enter_context(tc.psum_pool(name="scores%d" % g, bufs=3)) for g in range(2)]
+        score_pools = [ctx.enter_context(tc.psum_pool(name="scores%d" % g, bufs=SCORE_BANKS)) for g in range(2)]
         y_pool = ctx.enter_context(tc.psum_pool(name="y", bufs=2))
         ctx.enter_context(tc.manual_schedule())
-        tiles = {}
 
-        def new(key, shape, dtype):
-            tiles[key] = sb.tile(shape, dtype, name="_".join([str(x) for x in key]), align_bytes=64)
-            return tiles[key]
+        def tile(name, shape, dtype):
+            return sb.tile(shape, dtype, name=name, align_bytes=64)
 
-        def engine(name):
-            return {"sp": nc.sync, "act": nc.scalar, "pool": nc.gpsimd}[name]
-
-        k_codes = new(("k_codes",), [P, N], U32)
-        k_scales = new(("k_scales",), [P, N], U8)
-        k_words = new(("k_words",), [P, PACK, P, PACK], BF16)
-        q_of_block = {}
-        u_of_block = {}
-        y_of_block = {}
-        banks = {}
-
-        def quantize(codes, scales, words):
+        def quantise(codes, scales, words):
             nc.vector.quantize_mx(out=codes.bitcast(FP8X4), scales=scales, in_=words)
 
-        for op in plan():
-            kind = op[0]
-            if kind == "small":
-                t_col = new(("t",), [P, PACK], F32)
-                kb_col = new(("kb",), [P, PACK], F32)
-                kb_half = new(("kbh",), [P, PACK], F32)
-                nc.gpsimd.dma_start(out=kb_col[:], in_=kb.rearrange("(s r) o -> s (r o)", r=PACK))
-                nc.gpsimd.dma_start(out=t_col[:], in_=t.rearrange("(s r) o -> s (r o)", r=PACK))
-                nc.gpsimd.tensor_scalar(out=kb_half[:], in0=kb_col[:], scalar1=0.5, scalar2=0.0, op0=ALU.mult, op1=ALU.add)
-            elif kind == "warm":
-                warm_in = new(("warm_in",), [P, 1], F32)
-                warm_out = new(("warm_out",), [P, 1], F32)
-                nc.vector.memset(warm_in[:], 0.0)
-                nc.scalar.activation(out=warm_out[:], in_=warm_in[:], func=ACT.Sigmoid)
-            elif kind == "ld_q":
-                pair, b0, nb, g, eng = op[1:]
-                key = ("q_raw", pair, b0)
-                raw = tiles[key] if key in tiles else new(key, [P, PACK, nb * QB], F32)
-                cols = slice(b0 * QB, (b0 + nb) * QB)
-                if g == 2:
-                    src = qT[2 * pair : 2 * pair + 2, :, cols].rearrange("h (p j) q -> (h p) j q", j=PACK)
-                    engine(eng).dma_start(out=raw[:], in_=src)
-                else:
-                    src = qT[2 * pair + g, :, cols].rearrange("(p j) q -> p j q", j=PACK)
-                    engine(eng).dma_start(out=raw[ROWS * g : ROWS * (g + 1)], in_=src)
-            elif kind == "ld_k":
-                s0, s1, g, eng = op[1:]
-                key = ("k_raw", s0)
-                raw = tiles[key] if key in tiles else new(key, [P, PACK, (s1 - s0) * PACK], F32)
-                src = kT[0, :, s0 * PACK : s1 * PACK].rearrange("(p j) i -> p j i", j=PACK)
-                engine(eng).dma_start(out=raw[ROWS * g : ROWS * (g + 1)], in_=src)
-            elif kind == "ld_v":
-                raw = new(("v_raw",), [P, PACK, E], F32)
-                nc.sync.dma_start(out=raw[:], in_=v[0].rearrange("(s r) e -> s r e", r=PACK))
-            elif kind == "ld_og":
-                h = op[1]
-                raw = new(("og", h), [P, NQ // QB, E], F32)
-                nc.sync.dma_start(out=raw[:], in_=og[h].rearrange("(b p) e -> p b e", p=QB))
-            elif kind == "cp_k":
-                s0, s1 = op[1:]
-                raw = tiles[("k_raw", s0)]
-                nc.vector.tensor_copy(
-                    out=k_words[:, :, s0:s1, :].rearrange("p r s j -> p s j r"),
-                    in_=raw[:].rearrange("p j (s r) -> p s j r", r=PACK),
-                )
-            elif kind == "qz_k":
-                r0, r1 = op[1:]
-                cols = slice(r0 * P, r1 * P)
-                quantize(k_codes[:, cols], k_scales[:, cols], k_words[:, r0:r1].rearrange("p r s j -> p (r s j)"))
-            elif kind == "cp_q":
-                pair, b0, nb = op[1:]
-                raw = tiles[("q_raw", pair, b0)]
-                words = new(("q_words", pair, b0), [P, nb * QB, PACK], BF16)
-                nc.vector.tensor_copy(
-                    out=words[:].rearrange("p (c i) j -> p c j i", i=RUN),
-                    in_=raw[:].rearrange("p j (c i) -> p c j i", i=RUN),
-                )
-            elif kind == "qz_q":
-                pair, c0, b0, nb = op[1:]
-                words = tiles[("q_words", pair, c0)]
-                codes = new(("q_codes", pair, b0), [P, nb * QB], U32)
-                scales = new(("q_scales", pair, b0), [P, nb * QB], U8)
-                quantize(codes[:], scales[:], words[:, (b0 - c0) * QB : (b0 - c0 + nb) * QB, :].rearrange("p q j -> p (q j)"))
-                for b in range(nb):
-                    q_of_block[(pair, b0 + b)] = (codes, scales, slice(b * QB, (b + 1) * QB))
-            elif kind == "cp_v":
-                words = new(("v_words",), [P, E, PACK], BF16)
-                nc.vector.tensor_copy(
-                    out=words[:].rearrange("p (c i) r -> p c r i", i=RUN),
-                    in_=tiles[("v_raw",)][:].rearrange("p r (c i) -> p c r i", i=RUN),
-                )
-            elif kind == "qz_v":
-                v_codes = new(("v_codes",), [P, E], U32)
-                v_scales = new(("v_scales",), [P, E], U8)
-                quantize(v_codes[:], v_scales[:], tiles[("v_words",)][:].rearrange("p e r -> p (e r)"))
-            elif kind == "mm_s":
-                h, b0, nb, r0, r1 = op[1:]
-                g = h % 2
-                rows = slice(ROWS * g, ROWS * (g + 1))
-                bank = score_pools[g].tile([P, NQ], F32, name="bank", tag="bank")
-                for r in range(r0, r1):
-                    banks[(h, b0, r)] = bank[:, (r - r0) * nb * QB : (r - r0 + 1) * nb * QB]
-                    for b in range(nb):
-                        codes, scales, cols = q_of_block[(h // 2, b0 + b)]
-                        at = ((r - r0) * nb + b) * QB
+        def interleave(words, rows):
+            nc.vector.tensor_copy(
+                out=words.rearrange("p (c i) j -> p c j i", i=COPY_RUN),
+                in_=rows.rearrange("p j (c i) -> p c j i", i=COPY_RUN),
+            )
+
+        k_mx = tile("k_mx", [P, N + N // 4], I32)
+        k_codes = k_mx[:, 0:N]
+        k_scales = k_mx[:, N : N + N // 4].bitcast(U8)
+        k_words = tile("k_words", [ROWS, PACK, P, PACK], BF16)
+        k_raw = [tile("k_raw%d" % s0, [ROWS, PACK, (s1 - s0) * PACK], F32) for s0, s1 in K_PIECES]
+        v_raw = tile("v_raw", [P, PACK, E], F32)
+        v_words = tile("v_words", [P, E, PACK], BF16)
+        v_codes = tile("v_codes", [P, E], U32)
+        v_scales = tile("v_scales", [P, E], U8)
+        t_col = tile("t_col", [P, PACK], F32)
+        kb_col = tile("kb_col", [P, PACK], F32)
+        kb_half = tile("kb_half", [P, PACK], F32)
+        og_raw = tile("og_raw", [P, H * BLOCKS, E], F32)
+        gate = tile("gate", [P, H * BLOCKS, E], F32)
+        w_codes = [tile("w_codes%d" % h, [P, NQ], U32) for h in range(H)]
+        w_scales = [tile("w_scales%d" % h, [P, NQ], U8) for h in range(H)]
+
+        q_raw, q_words, q_mx = {}, {}, {}
+        score_at, capped_at, p_tiles, w_words, y_tiles = {}, {}, {}, {}, {}
+
+        def load_q(pair, block, count):
+            raw = tile("q_raw%d_%d" % (pair, block), [P, PACK, count * QB], F32)
+            src = qT[2 * pair : 2 * pair + 2, :, block * QB : (block + count) * QB]
+            nc.sync.dma_start(out=raw[:], in_=src.rearrange("h (p j) q -> (h p) j q", j=PACK))
+            q_raw[(pair, block)] = raw
+
+        def load_og(engine, h, block, count):
+            src = og[h, block * QB : (block + count) * QB, :].rearrange("(b p) e -> p b e", p=QB)
+            engine.dma_start(out=og_raw[:, BLOCKS * h + block : BLOCKS * h + block + count], in_=src)
+
+        def interleave_q(pair, block):
+            raw = q_raw[(pair, block)]
+            words = tile("q_words%d_%d" % (pair, block), [P, raw.shape[2], PACK], BF16)
+            interleave(words[:], raw[:])
+            q_words[(pair, block)] = words
+
+        def quantise_q(pair, block):
+            words = q_words[(pair, block)]
+            width = words.shape[1]
+            codes = tile("q_codes%d_%d" % (pair, block), [P, width], U32)
+            scales = tile("q_scales%d_%d" % (pair, block), [P, width], U8)
+            quantise(codes[:], scales[:], words[:].rearrange("p q j -> p (q j)"))
+            for b in range(width // QB):
+                q_mx[(pair, block + b)] = (codes, scales, slice(b * QB, (b + 1) * QB))
+
+        def scores(heads, block, count, places):
+            banks = [score_pools[h % 2].tile([P, BANK], F32, name="bank", tag="bank") for h in heads]
+            for n, r in enumerate(places):
+                keys = slice(r * P, (r + 1) * P)
+                for b in range(count):
+                    at = (n * count + b) * QB
+                    for h, bank in zip(heads, banks):
+                        rows = slice(ROWS * (h % 2), ROWS * (h % 2 + 1))
+                        codes, scales, cols = q_mx[(h // 2, block + b)]
+                        score_at[(h, block + b, r)] = (bank, at)
                         nc.tensor.matmul_mx(
                             out=bank[:, at : at + QB],
-                            lhsT=k_codes[rows, r * P : (r + 1) * P].bitcast(FP8X4),
-                            lhsT_scale=k_scales[rows, r * P : (r + 1) * P],
+                            lhsT=k_codes[rows, keys].bitcast(FP8X4),
+                            lhsT_scale=k_scales[rows, keys],
                             rhs=codes[rows, cols].bitcast(FP8X4),
                             rhs_scale=scales[rows, cols],
                             start=True,
                             stop=True,
                         )
-            elif kind == "T":
-                h, b0, nb, r = op[1:]
-                key = ("u", h, b0)
-                u = tiles[key] if key in tiles else new(key, [P, PACK, nb * QB], F32)
-                for b in range(nb):
-                    u_of_block[(h, b0 + b)] = (u, b * QB)
+
+        def cap(h, block, count, places):
+            if (h, block) not in capped_at:
+                capped = tile("capped%d_%d" % (h, block), [P, PACK, count * QB], F32)
+                for b in range(count):
+                    capped_at[(h, block + b)] = (capped, b * QB)
+            capped = capped_at[(h, block)][0]
+            for r in places:
+                bank, at = score_at[(h, block, r)]
                 nc.scalar.activation(
-                    out=u[:, r, :], in_=banks[(h, b0, r)], func=ACT.Tanh, bias=tiles[("kbh",)][:, r : r + 1], scale=0.5
+                    out=capped[:, r, :],
+                    in_=bank[:, at : at + count * QB],
+                    func=ACT.Tanh,
+                    bias=kb_half[:, r : r + 1],
+                    scale=0.5,
                 )
-            elif kind == "S":
-                h, b0, nb = op[1:]
-                u, at = u_of_block[(h, b0)]
-                p = new(("p", h, b0), [P, PACK, nb * QB], F32)
-                nc.scalar.activation(out=p[:], in_=u[:, :, at : at + nb * QB], func=ACT.Sigmoid, scale=2.0)
-            elif kind == "G":
-                h, b0, nb = op[1:]
-                key = ("gate", h)
-                gate = tiles[key] if key in tiles else new(key, [P, NQ // QB, E], F32)
-                nc.scalar.activation(out=gate[:, b0 : b0 + nb], in_=tiles[("og", h)][:, b0 : b0 + nb], func=ACT.Sigmoid)
-            elif kind == "W":
-                h, b0, nb = op[1:]
-                words = new(("w_words", h, b0), [P, nb * QB, PACK], BF16)
-                nc.vector.tensor_tensor(
-                    out=words[:].rearrange("p (c i) r -> p c r i", i=RUN),
-                    in0=tiles[("p", h, b0)][:].rearrange("p r (c i) -> p c r i", i=RUN),
-                    in1=tiles[("t",)][:].unsqueeze(1).unsqueeze(3).to_broadcast([P, nb * QB // RUN, PACK, RUN]),
-                    op=ALU.mult,
-                )
-            elif kind == "Q":
-                h, b0, nb = op[1:]
-                codes = new(("w_codes", h, b0), [P, nb * QB], U32)
-                scales = new(("w_scales", h, b0), [P, nb * QB], U8)
-                quantize(codes[:], scales[:], tiles[("w_words", h, b0)][:].rearrange("p q r -> p (q r)"))
-                for b in range(nb):
-                    tiles[("w", h, b0 + b)] = (codes, scales, slice(b * QB, (b + 1) * QB))
-            elif kind == "mm_y":
-                h, f0, b = op[1:]
-                if b == f0:
-                    y_of_block[(h, f0)] = y_pool.tile([P, NQ // QB, E], F32, name="y", tag="y")
-                codes, scales, cols = tiles[("w", h, b)]
+
+        def sigmoid(h, row, rows):
+            capped, at = capped_at[(h, row // QB)]
+            at = at + row % QB
+            p = tile("p%d_%d" % (h, row), [P, PACK, rows], F32)
+            nc.scalar.activation(out=p[:], in_=capped[:, :, at : at + rows], func=ACT.Sigmoid, scale=2.0)
+            p_tiles[(h, row)] = p
+
+        def gates(first, count):
+            nc.scalar.activation(
+                out=gate[:, first : first + count], in_=og_raw[:, first : first + count], func=ACT.Sigmoid
+            )
+
+        def weigh(h, row):
+            p = p_tiles[(h, row)]
+            rows = p.shape[2]
+            words = tile("w_words%d_%d" % (h, row), [P, rows, PACK], BF16)
+            nc.vector.tensor_tensor(
+                out=words[:].rearrange("p (c i) r -> p c r i", i=WEIGHT_RUN),
+                in0=p[:].rearrange("p r (c i) -> p c r i", i=WEIGHT_RUN),
+                in1=t_col[:].unsqueeze(1).unsqueeze(3).to_broadcast([P, rows // WEIGHT_RUN, PACK, WEIGHT_RUN]),
+                op=ALU.mult,
+            )
+            w_words[(h, row)] = words
+
+        def quantise_w(h, row):
+            words = w_words[(h, row)]
+            cols = slice(row, row + words.shape[1])
+            quantise(w_codes[h][:, cols], w_scales[h][:, cols], words[:].rearrange("p q r -> p (q r)"))
+
+        def values(h, block, count):
+            y = y_pool.tile([P, BLOCKS, E], F32, name="y", tag="y")
+            for b in range(count):
+                cols = slice((block + b) * QB, (block + b + 1) * QB)
                 nc.tensor.matmul_mx(
-                    out=y_of_block[(h, f0)][:, b - f0, :],
-                    lhsT=codes[:, cols].bitcast(FP8X4),
-                    lhsT_scale=scales[:, cols],
-                    rhs=tiles[("v_codes",)][:].bitcast(FP8X4),
-                    rhs_scale=tiles[("v_scales",)][:],
+                    out=y[:, b, :],
+                    lhsT=w_codes[h][:, cols].bitcast(FP8X4),
+                    lhsT_scale=w_scales[h][:, cols],
+                    rhs=v_codes[:].bitcast(FP8X4),
+                    rhs_scale=v_scales[:],
                     start=True,
                     stop=True,
                 )
-            elif kind == "F":
-                h, f0, nb = op[1:]
-                res = new(("res", h, f0), [P, nb, E], F32)
-                nc.vector.scalar_tensor_tensor(
-                    out=res[:],
-                    in0=y_of_block[(h, f0)][:, 0:nb, :],
-                    scalar=1.0 / 16.0,
-                    in1=tiles[("gate", h)][:, f0 : f0 + nb, :],
-                    op0=ALU.mult,
-                    op1=ALU.mult,
+            y_tiles[(h, block)] = (y, count)
+
+        def finish(h, block, engine):
+            y, count = y_tiles[(h, block)]
+            res = tile("res%d_%d" % (h, block), [P, count, E], F32)
+            first = BLOCKS * h + block
+            nc.vector.scalar_tensor_tensor(
+                out=res[:],
+                in0=y[:, 0:count, :],
+                scalar=1.0 / 16.0,
+                in1=gate[:, first : first + count, :],
+                op0=ALU.mult,
+                op1=ALU.mult,
+            )
+            dst = out[h, block * QB : (block + count) * QB, :].rearrange("(b p) e -> p b e", p=QB)
+            engine.dma_start(out=dst, in_=res[:])
+
+        load_q(0, 0, 1)
+        nc.scalar.dma_start(out=kb_col[:], in_=kb.rearrange("(s r) o -> s (r o)", r=PACK))
+        load_og(nc.scalar, 0, 0, 1)
+        for (s0, s1), raw in zip(K_PIECES, k_raw):
+            src = kT[0, :, s0 * PACK : s1 * PACK].rearrange("(p j) i -> p j i", j=PACK)
+            nc.sync.dma_start(out=raw[:], in_=src)
+        load_q(0, 1, 1)
+        load_og(nc.sync, 0, 1, BLOCKS - 1)
+        nc.sync.dma_start(out=t_col[:], in_=t.rearrange("(s r) o -> s (r o)", r=PACK))
+        load_q(0, 2, 2)
+
+        gates(0, 1)
+
+        nc.vector.memset(k_mx[0:ROWS, N : N + N // 4], 0)
+        nc.vector.tensor_scalar(out=kb_half[:], in0=kb_col[:], scalar1=0.5, scalar2=None, op0=ALU.mult)
+        interleave_q(0, 0)
+        quantise_q(0, 0)
+        for (s0, s1), raw in zip(K_PIECES, k_raw):
+            for r in (0, 2):
+                nc.vector.tensor_copy(
+                    out=k_words[:, r : r + 2, s0:s1, :].rearrange("p r s j -> p s r j"),
+                    in_=raw[:].rearrange("p j (s r) -> p s r j", r=PACK)[:, :, r : r + 2, :],
                 )
-                nc.sync.dma_start(
-                    out=out[h, f0 * QB : (f0 + nb) * QB, :].rearrange("(b p) e -> p b e", p=QB), in_=res[:]
-                )
+        for r in range(PACK):
+            keys = slice(r * P, (r + 1) * P)
+            quantise(k_codes[0:ROWS, keys], k_scales[0:ROWS, keys], k_words[:, r].rearrange("p s j -> p (s j)"))
+        nc.sync.dma_start(out=k_mx[ROWS:P, :], in_=k_mx[0:ROWS, :])
+
+        nc.sync.dma_start(out=v_raw[:], in_=v[0].rearrange("(s r) e -> s r e", r=PACK))
+        load_q(1, 0, 2)
+        load_og(nc.sync, 1, 0, BLOCKS)
+        load_q(1, 2, 2)
+        load_og(nc.sync, 2, 0, BLOCKS)
+        load_og(nc.sync, 3, 0, BLOCKS)
+
+        for places in ((0,), (1,), (2, 3)):
+            scores((0,), 0, 1, places)
+        interleave_q(0, 1)
+        quantise_q(0, 1)
+        cap(0, 0, 1, (0, 1, 2, 3))
+        scores((0,), 1, 1, (0, 1, 2, 3))
+        sigmoid(0, 0, QB)
+        interleave_q(0, 2)
+        weigh(0, 0)
+        quantise_q(0, 2)
+        quantise_w(0, 0)
+        cap(0, 1, 1, (3, 2, 1, 0))
+        gates(1, BLOCKS - 1)
+        sigmoid(0, QB, QB)
+        interleave(v_words[:], v_raw[:])
+        weigh(0, QB)
+        quantise(v_codes[:], v_scales[:], v_words[:].rearrange("p e r -> p (e r)"))
+
+        scores((1,), 0, 2, (0, 1))
+        scores((1,), 0, 2, (2, 3))
+        scores((1, 0), 2, 2, (0, 1))
+        interleave_q(1, 0)
+        quantise_w(0, QB)
+        quantise_q(1, 0)
+        interleave_q(1, 2)
+        cap(1, 0, 2, (1, 0, 3, 2))
+        scores((1, 0), 2, 2, (2, 3))
+        cap(0, 2, 2, (1, 0))
+        sigmoid(1, 0, 2 * QB)
+        weigh(1, 0)
+        quantise_q(1, 2)
+        quantise_w(1, 0)
+        scores((3, 2), 0, 2, (0, 1))
+        cap(1, 2, 2, (1, 0))
+        scores((3, 2), 0, 2, (2, 3))
+        for h in (0, 1):
+            cap(h, 2, 2, (3, 2))
+        scores((3, 2), 2, 2, (0, 1))
+        for h in (0, 1):
+            sigmoid(h, 2 * QB, 2 * QB)
+            weigh(h, 2 * QB)
+        for h in (0, 1):
+            quantise_w(h, 2 * QB)
+        values(0, 0, BLOCKS)
+        finish(0, 0, nc.sync)
+
+        for h in (2, 3):
+            cap(h, 0, 2, (1, 0))
+        scores((3, 2), 2, 2, (2, 3))
+        values(1, 0, BLOCKS)
+        for h in (2, 3):
+            cap(h, 0, 2, (3, 2))
+        for h in (2, 3):
+            sigmoid(h, 0, 2 * QB)
+            weigh(h, 0)
+        for h in (2, 3):
+            quantise_w(h, 0)
+        gates(BLOCKS, BLOCKS + 2)
+        finish(1, 0, nc.sync)
+        values(2, 0, 2)
+        finish(2, 0, nc.sync)
+
+        cap(2, 2, 2, (3, 2, 1, 0))
+        cap(3, 2, 1, (3, 2))
+        for row in (2 * QB, 3 * QB):
+            sigmoid(2, row, QB)
+            weigh(2, row)
+        for row in (2 * QB, 3 * QB):
+            quantise_w(2, row)
+        values(2, 2, 2)
+        cap(3, 2, 1, (1, 0))
+        cap(3, 3, 1, (3, 2))
+        sigmoid(3, 2 * QB, QB)
+        weigh(3, 2 * QB)
+        cap(3, 3, 1, (1, 0))
+        gates(2 * BLOCKS + 2, 2)
+        finish(2, 2, nc.sync)
+        quantise_w(3, 2 * QB)
+        values(3, 0, 3)
+        last_rows = (3 * QB, 3 * QB + QB // 2)
+        for row in last_rows:
+            sigmoid(3, row, QB // 2)
+            weigh(3, row)
+        gates(3 * BLOCKS, BLOCKS)
+        for row in last_rows:
+            quantise_w(3, row)
+        values(3, 3, 1)
+        finish(3, 0, nc.sync)
+        finish(3, 3, nc.scalar)

from contextlib import ExitStack

import concourse.mybir as mybir

H, D, NQ, N, E = 4, 256, 512, 512, 128
FLOPS = 2 * H * N * NQ * D + 2 * H * NQ * N * E

F32 = mybir.dt.float32
BF16 = mybir.dt.bfloat16
I32 = mybir.dt.int32
U32 = mybir.dt.uint32
U8 = mybir.dt.uint8
FP8X4 = mybir.dt.float8_e4m3fn_x4
ACT = mybir.ActivationFunctionType
ALU = mybir.AluOpType

P = 128
ROWS = D // 4
PACK = 4
QB = 128
BLOCKS = NQ // QB
BANK = 512
SCORE_BANKS = 3
K_PIECES = ((0, 64), (64, 104), (104, 128))
COPY_RUN = 4
WEIGHT_RUN = 2


def tile_rows_a_sigmoid_kb_cap_gate_kernel(tc, qT, kT, t, v, kb, og, out):
    nc = tc.nc
    with ExitStack() as ctx:
        sb = ctx.enter_context(tc.tile_pool(name="sb", bufs=1))
        score_pools = [ctx.enter_context(tc.psum_pool(name="scores%d" % g, bufs=SCORE_BANKS)) for g in range(2)]
        y_pool = ctx.enter_context(tc.psum_pool(name="y", bufs=2))
        ctx.enter_context(tc.manual_schedule())

        def tile(name, shape, dtype):
            return sb.tile(shape, dtype, name=name, align_bytes=64)

        def quantise(codes, scales, words):
            nc.vector.quantize_mx(out=codes.bitcast(FP8X4), scales=scales, in_=words)

        def interleave(words, rows):
            nc.vector.tensor_copy(
                out=words.rearrange("p (c i) j -> p c j i", i=COPY_RUN),
                in_=rows.rearrange("p j (c i) -> p c j i", i=COPY_RUN),
            )

        k_mx = tile("k_mx", [P, N + N // 4], I32)
        k_codes = k_mx[:, 0:N]
        k_scales = k_mx[:, N : N + N // 4].bitcast(U8)
        k_words = tile("k_words", [ROWS, PACK, P, PACK], BF16)
        k_raw = [tile("k_raw%d" % s0, [ROWS, PACK, (s1 - s0) * PACK], F32) for s0, s1 in K_PIECES]
        v_raw = tile("v_raw", [P, PACK, E], F32)
        v_words = tile("v_words", [P, E, PACK], BF16)
        v_codes = tile("v_codes", [P, E], U32)
        v_scales = tile("v_scales", [P, E], U8)
        t_col = tile("t_col", [P, PACK], F32)
        kb_col = tile("kb_col", [P, PACK], F32)
        kb_half = tile("kb_half", [P, PACK], F32)
        og_raw = tile("og_raw", [P, H * BLOCKS, E], F32)
        gate = tile("gate", [P, H * BLOCKS, E], F32)
        w_codes = [tile("w_codes%d" % h, [P, NQ], U32) for h in range(H)]
        w_scales = [tile("w_scales%d" % h, [P, NQ], U8) for h in range(H)]

        q_raw, q_words, q_mx = {}, {}, {}
        score_at, capped_at, p_tiles, w_words, y_tiles = {}, {}, {}, {}, {}

        def load_q(pair, block, count):
            raw = tile("q_raw%d_%d" % (pair, block), [P, PACK, count * QB], F32)
            src = qT[2 * pair : 2 * pair + 2, :, block * QB : (block + count) * QB]
            nc.sync.dma_start(out=raw[:], in_=src.rearrange("h (p j) q -> (h p) j q", j=PACK))
            q_raw[(pair, block)] = raw

        def load_og(engine, h, block, count):
            src = og[h, block * QB : (block + count) * QB, :].rearrange("(b p) e -> p b e", p=QB)
            engine.dma_start(out=og_raw[:, BLOCKS * h + block : BLOCKS * h + block + count], in_=src)

        def interleave_q(pair, block):
            raw = q_raw[(pair, block)]
            words = tile("q_words%d_%d" % (pair, block), [P, raw.shape[2], PACK], BF16)
            interleave(words[:], raw[:])
            q_words[(pair, block)] = words

        def quantise_q(pair, block):
            words = q_words[(pair, block)]
            width = words.shape[1]
            codes = tile("q_codes%d_%d" % (pair, block), [P, width], U32)
            scales = tile("q_scales%d_%d" % (pair, block), [P, width], U8)
            quantise(codes[:], scales[:], words[:].rearrange("p q j -> p (q j)"))
            for b in range(width // QB):
                q_mx[(pair, block + b)] = (codes, scales, slice(b * QB, (b + 1) * QB))

        def scores(heads, block, count, places):
            banks = [score_pools[h % 2].tile([P, BANK], F32, name="bank", tag="bank") for h in heads]
            for n, r in enumerate(places):
                keys = slice(r * P, (r + 1) * P)
                for b in range(count):
                    at = (n * count + b) * QB
                    for h, bank in zip(heads, banks):
                        rows = slice(ROWS * (h % 2), ROWS * (h % 2 + 1))
                        codes, scales, cols = q_mx[(h // 2, block + b)]
                        score_at[(h, block + b, r)] = (bank, at)
                        nc.tensor.matmul_mx(
                            out=bank[:, at : at + QB],
                            lhsT=k_codes[rows, keys].bitcast(FP8X4),
                            lhsT_scale=k_scales[rows, keys],
                            rhs=codes[rows, cols].bitcast(FP8X4),
                            rhs_scale=scales[rows, cols],
                            start=True,
                            stop=True,
                        )

        def cap(h, block, count, places):
            if (h, block) not in capped_at:
                capped = tile("capped%d_%d" % (h, block), [P, PACK, count * QB], F32)
                for b in range(count):
                    capped_at[(h, block + b)] = (capped, b * QB)
            capped = capped_at[(h, block)][0]
            for r in places:
                bank, at = score_at[(h, block, r)]
                nc.scalar.activation(
                    out=capped[:, r, :],
                    in_=bank[:, at : at + count * QB],
                    func=ACT.Tanh,
                    bias=kb_half[:, r : r + 1],
                    scale=0.5,
                )

        def sigmoid(h, row, rows):
            capped, at = capped_at[(h, row // QB)]
            at = at + row % QB
            p = tile("p%d_%d" % (h, row), [P, PACK, rows], F32)
            nc.scalar.activation(out=p[:], in_=capped[:, :, at : at + rows], func=ACT.Sigmoid, scale=2.0)
            p_tiles[(h, row)] = p

        def gates(first, count):
            nc.scalar.activation(
                out=gate[:, first : first + count], in_=og_raw[:, first : first + count], func=ACT.Sigmoid
            )

        def weigh(h, row):
            p = p_tiles[(h, row)]
            rows = p.shape[2]
            words = tile("w_words%d_%d" % (h, row), [P, rows, PACK], BF16)
            nc.vector.tensor_tensor(
                out=words[:].rearrange("p (c i) r -> p c r i", i=WEIGHT_RUN),
                in0=p[:].rearrange("p r (c i) -> p c r i", i=WEIGHT_RUN),
                in1=t_col[:].unsqueeze(1).unsqueeze(3).to_broadcast([P, rows // WEIGHT_RUN, PACK, WEIGHT_RUN]),
                op=ALU.mult,
            )
            w_words[(h, row)] = words

        def quantise_w(h, row):
            words = w_words[(h, row)]
            cols = slice(row, row + words.shape[1])
            quantise(w_codes[h][:, cols], w_scales[h][:, cols], words[:].rearrange("p q r -> p (q r)"))

        def values(h, block, count):
            y = y_pool.tile([P, BLOCKS, E], F32, name="y", tag="y")
            for b in range(count):
                cols = slice((block + b) * QB, (block + b + 1) * QB)
                nc.tensor.matmul_mx(
                    out=y[:, b, :],
                    lhsT=w_codes[h][:, cols].bitcast(FP8X4),
                    lhsT_scale=w_scales[h][:, cols],
                    rhs=v_codes[:].bitcast(FP8X4),
                    rhs_scale=v_scales[:],
                    start=True,
                    stop=True,
                )
            y_tiles[(h, block)] = (y, count)

        def finish(h, block, engine):
            y, count = y_tiles[(h, block)]
            res = tile("res%d_%d" % (h, block), [P, count, E], F32)
            first = BLOCKS * h + block
            nc.vector.scalar_tensor_tensor(
                out=res[:],
                in0=y[:, 0:count, :],
                scalar=1.0 / 16.0,
                in1=gate[:, first : first + count, :],
                op0=ALU.mult,
                op1=ALU.mult,
            )
            dst = out[h, block * QB : (block + count) * QB, :].rearrange("(b p) e -> p b e", p=QB)
            engine.dma_start(out=dst, in_=res[:])

        load_q(0, 0, 1)
        nc.scalar.dma_start(out=kb_col[:], in_=kb.rearrange("(s r) o -> s (r o)", r=PACK))
        load_og(nc.scalar, 0, 0, 1)
        for (s0, s1), raw in zip(K_PIECES, k_raw):
            src = kT[0, :, s0 * PACK : s1 * PACK].rearrange("(p j) i -> p j i", j=PACK)
            nc.sync.dma_start(out=raw[:], in_=src)
        load_q(0, 1, 1)
        load_og(nc.sync, 0, 1, BLOCKS - 1)
        nc.sync.dma_start(out=t_col[:], in_=t.rearrange("(s r) o -> s (r o)", r=PACK))
        load_q(0, 2, 2)

        gates(0, 1)

        nc.vector.memset(k_mx[0:ROWS, N : N + N // 4], 0)
        nc.vector.tensor_scalar(out=kb_half[:], in0=kb_col[:], scalar1=0.5, scalar2=None, op0=ALU.mult)
        interleave_q(0, 0)
        quantise_q(0, 0)
        for (s0, s1), raw in zip(K_PIECES, k_raw):
            for r in (0, 2):
                nc.vector.tensor_copy(
                    out=k_words[:, r : r + 2, s0:s1, :].rearrange("p r s j -> p s r j"),
                    in_=raw[:].rearrange("p j (s r) -> p s r j", r=PACK)[:, :, r : r + 2, :],
                )
        for r in range(PACK):
            keys = slice(r * P, (r + 1) * P)
            quantise(k_codes[0:ROWS, keys], k_scales[0:ROWS, keys], k_words[:, r].rearrange("p s j -> p (s j)"))
        nc.sync.dma_start(out=k_mx[ROWS:P, :], in_=k_mx[0:ROWS, :])

        nc.sync.dma_start(out=v_raw[:], in_=v[0].rearrange("(s r) e -> s r e", r=PACK))
        load_q(1, 0, 2)
        load_og(nc.sync, 1, 0, BLOCKS)
        load_q(1, 2, 2)
        load_og(nc.sync, 2, 0, BLOCKS)
        load_og(nc.sync, 3, 0, BLOCKS)

        for places in ((0,), (1,), (2, 3)):
            scores((0,), 0, 1, places)
        interleave_q(0, 1)
        quantise_q(0, 1)
        cap(0, 0, 1, (0, 1, 2, 3))
        scores((0,), 1, 1, (0, 1, 2, 3))
        sigmoid(0, 0, QB)
        interleave_q(0, 2)
        weigh(0, 0)
        quantise_q(0, 2)
        quantise_w(0, 0)
        cap(0, 1, 1, (3, 2, 1, 0))
        gates(1, BLOCKS - 1)
        sigmoid(0, QB, QB)
        interleave(v_words[:], v_raw[:])
        weigh(0, QB)
        quantise(v_codes[:], v_scales[:], v_words[:].rearrange("p e r -> p (e r)"))

        scores((1,), 0, 2, (0, 1))
        scores((1,), 0, 2, (2, 3))
        scores((1, 0), 2, 2, (0, 1))
        interleave_q(1, 0)
        quantise_w(0, QB)
        quantise_q(1, 0)
        interleave_q(1, 2)
        cap(1, 0, 2, (1, 0, 3, 2))
        scores((1, 0), 2, 2, (2, 3))
        cap(0, 2, 2, (1, 0))
        sigmoid(1, 0, 2 * QB)
        weigh(1, 0)
        quantise_q(1, 2)
        quantise_w(1, 0)
        scores((3, 2), 0, 2, (0, 1))
        cap(1, 2, 2, (1, 0))
        scores((3, 2), 0, 2, (2, 3))
        for h in (0, 1):
            cap(h, 2, 2, (3, 2))
        scores((3, 2), 2, 2, (0, 1))
        for h in (0, 1):
            sigmoid(h, 2 * QB, 2 * QB)
            weigh(h, 2 * QB)
        for h in (0, 1):
            quantise_w(h, 2 * QB)
        values(0, 0, BLOCKS)
        finish(0, 0, nc.sync)

        for h in (2, 3):
            cap(h, 0, 2, (1, 0))
        scores((3, 2), 2, 2, (2, 3))
        values(1, 0, BLOCKS)
        for h in (2, 3):
            cap(h, 0, 2, (3, 2))
        for h in (2, 3):
            sigmoid(h, 0, 2 * QB)
            weigh(h, 0)
        for h in (2, 3):
            quantise_w(h, 0)
        gates(BLOCKS, BLOCKS + 2)
        finish(1, 0, nc.sync)
        values(2, 0, 2)
        finish(2, 0, nc.sync)

        cap(2, 2, 2, (3, 2, 1, 0))
        cap(3, 2, 1, (3, 2))
        for row in (2 * QB, 3 * QB):
            sigmoid(2, row, QB)
            weigh(2, row)
        for row in (2 * QB, 3 * QB):
            quantise_w(2, row)
        values(2, 2, 2)
        cap(3, 2, 1, (1, 0))
        cap(3, 3, 1, (3, 2))
        sigmoid(3, 2 * QB, QB)
        weigh(3, 2 * QB)
        cap(3, 3, 1, (1, 0))
        gates(2 * BLOCKS + 2, 2)
        finish(2, 2, nc.sync)
        quantise_w(3, 2 * QB)
        values(3, 0, 3)
        last_rows = (3 * QB, 3 * QB + QB // 2)
        for row in last_rows:
            sigmoid(3, row, QB // 2)
            weigh(3, row)
        gates(3 * BLOCKS, BLOCKS)
        for row in last_rows:
            quantise_w(3, row)
        values(3, 3, 1)
        finish(3, 0, nc.sync)
        finish(3, 3, nc.scalar)
